import numpy as np
import ml_dtypes


def mxq(x, axis, fmt="e4m3"):
    dtype, down = {"e4m3": (ml_dtypes.float8_e4m3fn, 7), "e5m2": (ml_dtypes.float8_e5m2, 14)}[fmt]
    v = np.moveaxis(np.asarray(x, np.float32).astype(ml_dtypes.bfloat16).astype(np.float64), axis, -1)
    blocks = v.reshape(v.shape[:-1] + (-1, 32))
    amax = np.abs(blocks).max(-1, keepdims=True)
    byte = np.maximum(np.where(amax > 0, np.frexp(amax)[1] - 1 + 127, 0) - down, 1)
    scale = np.exp2(byte - 127.0)
    codes = (blocks / scale).astype(np.float32).astype(dtype).astype(np.float64)
    return np.moveaxis((codes * scale).reshape(v.shape), -1, axis)


WIDE = False


def mx_kscale(k):
    if not WIDE:
        return np.ones(k)
    levels = np.array([30, -30])
    if k % 512:
        return np.exp2(np.random.permutation(np.resize(levels, k // 32))).repeat(32)
    a = np.empty((k // 512, 16))
    for p in range(k // 512):
        a[p, :8] = np.random.permutation(np.resize(levels, 8))
        for g in range(8):
            far = levels[np.abs(levels - a[p, g]) >= 10]
            a[p, g + 8] = far[np.random.randint(len(far))]
    return np.exp2(a.ravel()).repeat(32)


def f64(x):
    return np.asarray(x).astype(np.float64)


def striped(idx):
    return np.tile(np.asarray(idx).reshape(-1, 16).T, (8, 1)).astype(np.uint16)


def unstriped(offs):
    return offs[:16].T.reshape(-1).astype(np.int64)


E2M1 = np.array([0.0, 0.5, 1.0, 1.5, 2.0, 3.0, 4.0, 6.0, -0.0, -0.5, -1.0, -1.5, -2.0, -3.0, -4.0, -6.0])


def pack_weight(w, fmt):
    k, n = w.shape
    w = f64(np.asarray(w, np.float32).astype(ml_dtypes.bfloat16)).reshape(k // 32, 32, n)
    amax = np.abs(w).max(1)
    if fmt in ("e4m3", "e5m2"):
        byte = np.frexp(amax)[1] - 1 + 127 - (7 if fmt == "e4m3" else 14)
    else:
        mant, ex = np.frexp(amax / 6.0)
        byte = np.where(mant > 0.5, ex, ex - 1) + 127
    byte = np.clip(np.where(amax > 0, byte, 1), 1, 254)
    scaled = (w * np.exp2(127.0 - byte)[:, None, :]).reshape(k, n).astype(np.float32)
    by_word = np.ascontiguousarray(scaled.reshape(k // 512, 128, 4, n).transpose(0, 1, 3, 2))
    if fmt in ("e4m3", "e5m2"):
        words = by_word.astype(ml_dtypes.float8_e4m3fn if fmt == "e4m3" else ml_dtypes.float8_e5m2).view(np.uint8)
    else:
        c = by_word.astype(ml_dtypes.float4_e2m1fn).view(np.uint8) & 0xF
        words = (c[..., 0::2] | (c[..., 1::2] << 4)).reshape(k // 512, 128, 2 * n)
    return np.ascontiguousarray(words), np.ascontiguousarray(byte.astype(np.uint8).reshape(k // 512, 16, n))


def unpack_weight(words, scales, fmt):
    g, _, n = scales.shape
    words = np.ascontiguousarray(words).reshape(g, 128, n, -1)
    if fmt in ("e4m3", "e5m2"):
        vals = words.view(ml_dtypes.float8_e4m3fn if fmt == "e4m3" else ml_dtypes.float8_e5m2).astype(np.float64)
    else:
        nib = np.empty((g, 128, n, 4), np.uint8)
        nib[..., 0::2] = words & 0xF
        nib[..., 1::2] = words >> 4
        vals = E2M1[nib]
    vals = vals * np.repeat(np.exp2(scales.astype(np.float64) - 127.0), 8, axis=1)[..., None]
    return vals.transpose(0, 1, 3, 2).reshape(g * 512, n)


K, Q, J, T, V, X, S, N, E = 512, 128, 256, 1024, 512, 1024, 512, 256, 512


def setup_inputs():
    n = np.random.standard_normal
    idx = np.random.permutation(T)[:J]
    idx2 = np.random.permutation(V)[:J]
    idx3 = np.random.permutation(X)[:J]
    idx4 = np.random.permutation(S)[:J]
    idx5 = np.random.permutation(E)[:J]
    fk = mx_kscale(K)
    wp = pack_weight(n((K, N)) * 1 / np.sqrt(K) / fk[:, None], "e5m2")
    return {
        "ca": (np.random.randint(-7, 8, (Q, T)).astype(np.float64)).astype(np.float32),
        "ga": (np.random.uniform(0.1, 0.4, (Q, 1)) * fk[::4, None]).astype(np.float32),
        "cb": (np.random.randint(-7, 8, (Q, V)).astype(np.float64)).astype(np.float32),
        "gb": (np.random.uniform(0.1, 0.4, (Q, 1)) * fk[::4, None]).astype(np.float32),
        "cc": (np.random.randint(-7, 8, (Q, X)).astype(np.float64)).astype(np.float32),
        "gc": (np.random.uniform(0.1, 0.4, (Q, 1)) * fk[::4, None]).astype(np.float32),
        "cd": (np.random.randint(-7, 8, (Q, S)).astype(np.float64)).astype(np.float32),
        "gd": (np.random.uniform(0.1, 0.4, (Q, 1)) * fk[::4, None]).astype(np.float32),
        "w_words": wp[0],
        "w_scales": wp[1],
        "so": (np.random.uniform(0.5, 1.6, (N, 1))).astype(np.float32),
        "offs": striped(idx),
        "offs2": striped(idx2),
        "offs3": striped(idx3),
        "offs4": striped(idx4),
        "offs5": striped(idx5),
    }


def reference(ca, ga, cb, gb, cc, gc, cd, gd, w_words, w_scales, so, offs, offs2, offs3, offs4, offs5):
    idx = unstriped(offs)
    idx2 = unstriped(offs2)
    idx3 = unstriped(offs3)
    idx4 = unstriped(offs4)
    idx5 = unstriped(offs5)
    wu = unpack_weight(w_words, w_scales, "e5m2")
    v0 = f64(ca)[:, idx] * f64(ga)
    v1 = f64(cb)[:, idx2] * f64(gb)
    v2 = f64(cc)[:, idx3] * f64(gc)
    v3 = f64(cd)[:, idx4] * f64(gd)
    z = np.stack([v0, v1, v2, v3], axis=1).reshape(K, J)
    zq = mxq(z, 0, "e4m3")
    p = wu.T @ zq
    y = np.zeros((N, E))
    y[:, idx5] = p * f64(so)
    return y

@@ -1,0 +1,103 @@
+from contextlib import ExitStack
+
+import concourse.mybir as mybir
+
+K, J, N, E = 512, 256, 256, 512
+FLOPS = 2 * K * N * J
+
+F32 = mybir.dt.float32
+BF16 = mybir.dt.bfloat16
+I32 = mybir.dt.int32
+U16 = mybir.dt.uint16
+U8 = mybir.dt.uint8
+E4M3X4 = mybir.dt.float8_e4m3fn_x4
+E5M2X4 = mybir.dt.float8_e5m2_x4
+COPY = mybir.ActivationFunctionType.Copy
+
+P = 128
+PACK = 4
+ITEMS = 128
+LIST_ROWS = 16
+QUADRANT = 32
+SCALE_ROWS = 4
+LINE = 8
+
+
+def tile_list_fourtables_kernel(tc, ca, ga, cb, gb, cc, gc, cd, gd, w_words, w_scales, so,
+                                 offs, offs2, offs3, offs4, offs5, out):
+    nc = tc.nc
+    halves = range(J // ITEMS)
+    pages = range(N // P)
+    list_cols = ITEMS // LIST_ROWS
+
+    with ExitStack() as ctx:
+        sb = ctx.enter_context(tc.tile_pool(name="sb", bufs=1))
+        psum = ctx.enter_context(tc.psum_pool(name="psum", bufs=1))
+
+        def load(queue, src, dtype, name):
+            held = sb.tile(list(src.shape), dtype, name=name, align_bytes=64)
+            queue.dma_start(held[:], src)
+            return held
+
+        table, entries, step = {}, {}, {}
+        step[0] = load(nc.gpsimd, ga, F32, "step_a")
+        step[2] = load(nc.gpsimd, gc, F32, "step_c")
+        staged = sb.tile([SCALE_ROWS, P // QUADRANT, N // 4], I32, name="staged")
+        nc.gpsimd.dma_start(staged[:], w_scales[0].bitcast(I32).rearrange("(q r) c -> r q c", r=SCALE_ROWS))
+        weight = sb.tile([P, N // P, LINE], F32, name="weight")
+        with nc.allow_non_contiguous_dma(reason="one value a partition and page"):
+            nc.gpsimd.dma_start(weight[:, :, 0:1], so.rearrange("(c p) o -> p c o", p=P))
+
+        table[1] = load(nc.sync, cb, F32, "table_b")
+        entries[1] = load(nc.sync, offs2, U16, "entries_b")
+        step[1] = load(nc.sync, gb, F32, "step_b")
+        table[3] = load(nc.sync, cd, F32, "table_d")
+        entries[3] = load(nc.sync, offs4, U16, "entries_d")
+        step[3] = load(nc.sync, gd, F32, "step_d")
+        table[0] = load(nc.sync, ca, F32, "table_a")
+        entries[0] = load(nc.sync, offs, U16, "entries_a")
+        table[2] = load(nc.sync, cc, F32, "table_c")
+        entries[2] = load(nc.sync, offs3, U16, "entries_c")
+        w_codes = load(nc.sync, w_words[0].rearrange("p n t -> p (n t)").bitcast(I32), I32, "w_codes")
+        places = load(nc.sync, offs5, U16, "places")
+
+        w_plane = sb.tile([P, N], U8, name="w_plane", align_bytes=64)
+        nc.vector.memset(w_plane[:].bitcast(I32), 0)
+        page = [sb.tile([P, E], F32, name="page%d" % c) for c in pages]
+        for c in pages:
+            nc.vector.memset(page[c][:], 0.0)
+        for q in range(P // QUADRANT):
+            nc.vector.tensor_copy(w_plane[QUADRANT * q : QUADRANT * q + SCALE_ROWS, :].bitcast(I32), staged[:, q, :])
+
+        z = sb.tile([P, PACK * J], BF16, name="z", align_bytes=64)
+
+        def fetch(t, first, count):
+            picks = entries[t][:, first // LIST_ROWS : (first + count) // LIST_ROWS]
+            nc.scalar.activation(z[:, PACK * first + t : PACK * (first + count) : PACK],
+                                 table[t][:].indirect(picks), COPY, scale=step[t][:])
+
+        for t in (1, 3, 0):
+            fetch(t, 0, J)
+        for h in halves:
+            fetch(2, ITEMS * h, ITEMS)
+
+        product = {}
+        for h in halves:
+            z_codes = sb.tile([P, ITEMS], I32, name="z_codes%d" % h, align_bytes=64)
+            z_plane = sb.tile([P, ITEMS], U8, name="z_plane%d" % h, align_bytes=64)
+            nc.vector.quantize_mx(z_codes[:].bitcast(E4M3X4), z_plane[:],
+                                  z[:, PACK * ITEMS * h : PACK * ITEMS * (h + 1)])
+            for c in pages:
+                cols = slice(P * c, P * (c + 1))
+                acc = psum.tile([P, ITEMS], F32, name="acc%d_%d" % (h, c))
+                nc.tensor.matmul_mx(acc[:], lhsT=w_codes[:, cols].bitcast(E5M2X4), lhsT_scale=w_plane[:, cols],
+                                    rhs=z_codes[:].bitcast(E4M3X4), rhs_scale=z_plane[:], start=True, stop=True)
+                product[h, c] = sb.tile([P, ITEMS], F32, name="product%d_%d" % (h, c))
+                nc.vector.tensor_copy(product[h, c][:], acc[:])
+
+        for h in halves:
+            for c in pages:
+                nc.scalar.activation(page[c][:].indirect(places[:, list_cols * h : list_cols * (h + 1)]),
+                                     product[h, c][:], COPY, scale=weight[:, c, 0:1])
+        for c in pages:
+            nc.sync.dma_start(out[P * c : P * (c + 1), :], page[c][:])

@@ -39,6 +39,11 @@ def tile_list_fourtables_kernel(tc, ca, ga, cb, gb, cc, gc, cd, gd, w_words, w_s
             queue.dma_start(held[:], src)
             return held
 
+        warm_in = sb.tile([P, 1], F32, name="warm_in")
+        warm_out = sb.tile([P, 1], F32, name="warm_out")
+        nc.vector.memset(warm_in[:], 0.0)
+        nc.scalar.activation(warm_out[:], warm_in[:], COPY)
+
         table, entries, step = {}, {}, {}
         step[0] = load(nc.gpsimd, ga, F32, "step_a")
         step[2] = load(nc.gpsimd, gc, F32, "step_c")

@@ -45,25 +45,25 @@ def tile_list_fourtables_kernel(tc, ca, ga, cb, gb, cc, gc, cd, gd, w_words, w_s
         nc.scalar.activation(warm_out[:], warm_in[:], COPY)
 
         table, entries, step = {}, {}, {}
-        step[0] = load(nc.gpsimd, ga, F32, "step_a")
-        step[2] = load(nc.gpsimd, gc, F32, "step_c")
         staged = sb.tile([SCALE_ROWS, P // QUADRANT, N // 4], I32, name="staged")
         nc.gpsimd.dma_start(staged[:], w_scales[0].bitcast(I32).rearrange("(q r) c -> r q c", r=SCALE_ROWS))
         weight = sb.tile([P, N // P, LINE], F32, name="weight")
         with nc.allow_non_contiguous_dma(reason="one value a partition and page"):
             nc.gpsimd.dma_start(weight[:, :, 0:1], so.rearrange("(c p) o -> p c o", p=P))
 
-        table[1] = load(nc.sync, cb, F32, "table_b")
         entries[1] = load(nc.sync, offs2, U16, "entries_b")
         step[1] = load(nc.sync, gb, F32, "step_b")
-        table[3] = load(nc.sync, cd, F32, "table_d")
         entries[3] = load(nc.sync, offs4, U16, "entries_d")
+        table[1] = load(nc.scalar, cb, F32, "table_b")
+        table[3] = load(nc.scalar, cd, F32, "table_d")
+        table[0] = load(nc.scalar, ca, F32, "table_a")
+        table[2] = load(nc.scalar, cc, F32, "table_c")
+        w_codes = load(nc.scalar, w_words[0].rearrange("p n t -> p (n t)").bitcast(I32), I32, "w_codes")
         step[3] = load(nc.sync, gd, F32, "step_d")
-        table[0] = load(nc.sync, ca, F32, "table_a")
         entries[0] = load(nc.sync, offs, U16, "entries_a")
-        table[2] = load(nc.sync, cc, F32, "table_c")
+        step[0] = load(nc.sync, ga, F32, "step_a")
         entries[2] = load(nc.sync, offs3, U16, "entries_c")
-        w_codes = load(nc.sync, w_words[0].rearrange("p n t -> p (n t)").bitcast(I32), I32, "w_codes")
+        step[2] = load(nc.sync, gc, F32, "step_c")
         places = load(nc.sync, offs5, U16, "places")
 
         w_plane = sb.tile([P, N], U8, name="w_plane", align_bytes=64)
@@ -81,10 +81,11 @@ def tile_list_fourtables_kernel(tc, ca, ga, cb, gb, cc, gc, cd, gd, w_words, w_s
             nc.scalar.activation(z[:, PACK * first + t : PACK * (first + count) : PACK],
                                  table[t][:].indirect(picks), COPY, scale=step[t][:])
 
-        for t in (1, 3, 0):
+        for t in (1, 3):
             fetch(t, 0, J)
         for h in halves:
-            fetch(2, ITEMS * h, ITEMS)
+            for t in (0, 2):
+                fetch(t, ITEMS * h, ITEMS)
 
         product = {}
         for h in halves:

from contextlib import ExitStack

import concourse.mybir as mybir

K, J, N, E = 512, 256, 256, 512
FLOPS = 2 * K * N * J

F32 = mybir.dt.float32
BF16 = mybir.dt.bfloat16
I32 = mybir.dt.int32
U16 = mybir.dt.uint16
U8 = mybir.dt.uint8
E4M3X4 = mybir.dt.float8_e4m3fn_x4
E5M2X4 = mybir.dt.float8_e5m2_x4
COPY = mybir.ActivationFunctionType.Copy

P = 128
PACK = 4
ITEMS = 128
LIST_ROWS = 16
QUADRANT = 32
SCALE_ROWS = 4
LINE = 8


def tile_list_fourtables_kernel(tc, ca, ga, cb, gb, cc, gc, cd, gd, w_words, w_scales, so,
                                 offs, offs2, offs3, offs4, offs5, out):
    nc = tc.nc
    halves = range(J // ITEMS)
    pages = range(N // P)
    list_cols = ITEMS // LIST_ROWS

    with ExitStack() as ctx:
        sb = ctx.enter_context(tc.tile_pool(name="sb", bufs=1))
        psum = ctx.enter_context(tc.psum_pool(name="psum", bufs=1))

        def load(queue, src, dtype, name):
            held = sb.tile(list(src.shape), dtype, name=name, align_bytes=64)
            queue.dma_start(held[:], src)
            return held

        warm_in = sb.tile([P, 1], F32, name="warm_in")
        warm_out = sb.tile([P, 1], F32, name="warm_out")
        nc.vector.memset(warm_in[:], 0.0)
        nc.scalar.activation(warm_out[:], warm_in[:], COPY)

        table, entries, step = {}, {}, {}
        staged = sb.tile([SCALE_ROWS, P // QUADRANT, N // 4], I32, name="staged")
        nc.gpsimd.dma_start(staged[:], w_scales[0].bitcast(I32).rearrange("(q r) c -> r q c", r=SCALE_ROWS))
        weight = sb.tile([P, N // P, LINE], F32, name="weight")
        with nc.allow_non_contiguous_dma(reason="one value a partition and page"):
            nc.gpsimd.dma_start(weight[:, :, 0:1], so.rearrange("(c p) o -> p c o", p=P))

        entries[1] = load(nc.sync, offs2, U16, "entries_b")
        step[1] = load(nc.sync, gb, F32, "step_b")
        entries[3] = load(nc.sync, offs4, U16, "entries_d")
        table[1] = load(nc.scalar, cb, F32, "table_b")
        table[3] = load(nc.scalar, cd, F32, "table_d")
        table[0] = load(nc.scalar, ca, F32, "table_a")
        table[2] = load(nc.scalar, cc, F32, "table_c")
        w_codes = load(nc.scalar, w_words[0].rearrange("p n t -> p (n t)").bitcast(I32), I32, "w_codes")
        step[3] = load(nc.sync, gd, F32, "step_d")
        entries[0] = load(nc.sync, offs, U16, "entries_a")
        step[0] = load(nc.sync, ga, F32, "step_a")
        entries[2] = load(nc.sync, offs3, U16, "entries_c")
        step[2] = load(nc.sync, gc, F32, "step_c")
        places = load(nc.sync, offs5, U16, "places")

        w_plane = sb.tile([P, N], U8, name="w_plane", align_bytes=64)
        nc.vector.memset(w_plane[:].bitcast(I32), 0)
        page = [sb.tile([P, E], F32, name="page%d" % c) for c in pages]
        for c in pages:
            nc.vector.memset(page[c][:], 0.0)
        for q in range(P // QUADRANT):
            nc.vector.tensor_copy(w_plane[QUADRANT * q : QUADRANT * q + SCALE_ROWS, :].bitcast(I32), staged[:, q, :])

        z = sb.tile([P, PACK * J], BF16, name="z", align_bytes=64)

        def fetch(t, first, count):
            picks = entries[t][:, first // LIST_ROWS : (first + count) // LIST_ROWS]
            nc.scalar.activation(z[:, PACK * first + t : PACK * (first + count) : PACK],
                                 table[t][:].indirect(picks), COPY, scale=step[t][:])

        for t in (1, 3):
            fetch(t, 0, J)
        for h in halves:
            for t in (0, 2):
                fetch(t, ITEMS * h, ITEMS)

        product = {}
        for h in halves:
            z_codes = sb.tile([P, ITEMS], I32, name="z_codes%d" % h, align_bytes=64)
            z_plane = sb.tile([P, ITEMS], U8, name="z_plane%d" % h, align_bytes=64)
            nc.vector.quantize_mx(z_codes[:].bitcast(E4M3X4), z_plane[:],
                                  z[:, PACK * ITEMS * h : PACK * ITEMS * (h + 1)])
            for c in pages:
                cols = slice(P * c, P * (c + 1))
                acc = psum.tile([P, ITEMS], F32, name="acc%d_%d" % (h, c))
                nc.tensor.matmul_mx(acc[:], lhsT=w_codes[:, cols].bitcast(E5M2X4), lhsT_scale=w_plane[:, cols],
                                    rhs=z_codes[:].bitcast(E4M3X4), rhs_scale=z_plane[:], start=True, stop=True)
                product[h, c] = sb.tile([P, ITEMS], F32, name="product%d_%d" % (h, c))
                nc.vector.tensor_copy(product[h, c][:], acc[:])

        for h in halves:
            for c in pages:
                nc.scalar.activation(page[c][:].indirect(places[:, list_cols * h : list_cols * (h + 1)]),
                                     product[h, c][:], COPY, scale=weight[:, c, 0:1])
        for c in pages:
            nc.sync.dma_start(out[P * c : P * (c + 1), :], page[c][:])
